import numpy as np
import ml_dtypes


def mxq(x, axis, fmt="e4m3"):
    dtype, down = {"e4m3": (ml_dtypes.float8_e4m3fn, 7), "e5m2": (ml_dtypes.float8_e5m2, 14)}[fmt]
    v = np.moveaxis(np.asarray(x, np.float32).astype(ml_dtypes.bfloat16).astype(np.float64), axis, -1)
    blocks = v.reshape(v.shape[:-1] + (-1, 32))
    amax = np.abs(blocks).max(-1, keepdims=True)
    byte = np.maximum(np.where(amax > 0, np.frexp(amax)[1] - 1 + 127, 0) - down, 1)
    scale = np.exp2(byte - 127.0)
    codes = (blocks / scale).astype(np.float32).astype(dtype).astype(np.float64)
    return np.moveaxis((codes * scale).reshape(v.shape), -1, axis)


WIDE = False


def mx_kscale(k):
    if not WIDE:
        return np.ones(k)
    levels = np.array([10, -10, 5, -5, 0])
    if k % 512:
        return np.exp2(np.random.permutation(np.resize(levels, k // 32))).repeat(32)
    a = np.empty((k // 512, 16))
    for p in range(k // 512):
        a[p, :8] = np.random.permutation(np.resize(levels, 8))
        for g in range(8):
            far = levels[np.abs(levels - a[p, g]) >= 10]
            a[p, g + 8] = far[np.random.randint(len(far))]
    return np.exp2(a.ravel()).repeat(32)


def f64(x):
    return np.asarray(x).astype(np.float64)


def striped8(idx):
    return np.asarray(idx).reshape(8, -1, 16).transpose(0, 2, 1).reshape(128, -1).astype(np.uint16)


def unstriped8(offs):
    return offs.reshape(8, 16, -1).transpose(0, 2, 1).reshape(8, -1).astype(np.int64)


def pick8(x, idx, run):
    r = np.arange(len(x))
    return x[r[:, None], idx[r % (8 * run) // run]]


E2M1 = np.array([0.0, 0.5, 1.0, 1.5, 2.0, 3.0, 4.0, 6.0, -0.0, -0.5, -1.0, -1.5, -2.0, -3.0, -4.0, -6.0])


def pack_weight(w, fmt):
    k, n = w.shape
    w = f64(np.asarray(w, np.float32).astype(ml_dtypes.bfloat16)).reshape(k // 32, 32, n)
    amax = np.abs(w).max(1)
    if fmt == "e4m3":
        byte = np.frexp(amax)[1] - 1 + 127 - 7
    else:
        mant, ex = np.frexp(amax / 6.0)
        byte = np.where(mant > 0.5, ex, ex - 1) + 127
    byte = np.clip(np.where(amax > 0, byte, 1), 1, 254)
    scaled = (w * np.exp2(127.0 - byte)[:, None, :]).reshape(k, n).astype(np.float32)
    by_word = np.ascontiguousarray(scaled.reshape(k // 512, 128, 4, n).transpose(0, 1, 3, 2))
    if fmt == "e4m3":
        words = by_word.astype(ml_dtypes.float8_e4m3fn).view(np.uint8)
    else:
        c = by_word.astype(ml_dtypes.float4_e2m1fn).view(np.uint8) & 0xF
        words = (c[..., 0::2] | (c[..., 1::2] << 4)).reshape(k // 512, 128, 2 * n)
    return np.ascontiguousarray(words), np.ascontiguousarray(byte.astype(np.uint8).reshape(k // 512, 16, n))


def unpack_weight(words, scales, fmt):
    g, _, n = scales.shape
    words = np.ascontiguousarray(words).reshape(g, 128, n, -1)
    if fmt == "e4m3":
        vals = words.view(ml_dtypes.float8_e4m3fn).astype(np.float64)
    else:
        nib = np.empty((g, 128, n, 4), np.uint8)
        nib[..., 0::2] = words & 0xF
        nib[..., 1::2] = words >> 4
        vals = E2M1[nib]
    vals = vals * np.repeat(np.exp2(scales.astype(np.float64) - 127.0), 8, axis=1)[..., None]
    return vals.transpose(0, 1, 3, 2).reshape(g * 512, n)


D, K, T, I, Q = 512, 512, 1024, 512, 128


def setup_inputs():
    n = np.random.standard_normal
    idx = np.stack([np.random.permutation(T)[:I] for _ in range(8)])
    idx2 = np.stack([np.random.permutation(T)[:I] for _ in range(8)])
    idx3 = np.stack([np.random.permutation(T)[:I] for _ in range(8)])
    idx4 = np.stack([np.random.permutation(T)[:I] for _ in range(8)])
    idx5 = np.stack([np.random.permutation(T)[:I] for _ in range(8)])
    idx6 = np.stack([np.random.permutation(T)[:I] for _ in range(8)])
    fd = mx_kscale(D)
    fk = mx_kscale(K)
    wqp = pack_weight(n((D, K)) * 1.0 / np.sqrt(D) * fd[:, None] * fk, "e4m3")
    keysp = pack_weight(n((K, T)) * 1.0 / np.sqrt(K) / fk[:, None], "e4m3")
    tagsp = pack_weight(n((D, T)) * 0.5 / np.sqrt(D) * fd[:, None], "e2m1")
    return {
        "states": (n((D, Q)) * 0.95 / fd[:, None]).astype(np.float32),
        "wq_words": wqp[0],
        "wq_scales": wqp[1],
        "keys_words": keysp[0],
        "keys_scales": keysp[1],
        "tags_words": tagsp[0],
        "tags_scales": tagsp[1],
        "offs": striped8(idx),
        "offs2": striped8(idx2),
        "offs3": striped8(idx3),
        "offs4": striped8(idx4),
        "offs5": striped8(idx5),
        "offs6": striped8(idx6),
    }


def reference(states, wq_words, wq_scales, keys_words, keys_scales, tags_words, tags_scales, offs, offs2, offs3, offs4, offs5, offs6):
    idx = unstriped8(offs)
    idx2 = unstriped8(offs2)
    idx3 = unstriped8(offs3)
    idx4 = unstriped8(offs4)
    idx5 = unstriped8(offs5)
    idx6 = unstriped8(offs6)
    wqu = unpack_weight(wq_words, wq_scales, "e4m3")
    keysu = unpack_weight(keys_words, keys_scales, "e4m3")
    tagsu = unpack_weight(tags_words, tags_scales, "e2m1")
    statesq = mxq(f64(states), 0, "e4m3")
    qv = wqu.T @ statesq
    qvq = mxq(qv, 0, "e4m3")
    a = qvq.T @ keysu + statesq.T @ tagsu
    f1 = np.zeros((Q, T))
    f1[np.arange(Q)[:, None], idx2[np.arange(Q) % 128 // 16]] = pick8(a, idx, 16)
    c1 = a - f1
    w = np.maximum(pick8(c1, idx3, 16), pick8(a, idx, 16))
    f2 = np.zeros((Q, T))
    f2[np.arange(Q)[:, None], idx4[np.arange(Q) % 128 // 16]] = w
    c2 = c1 + f2
    y = pick8(c2, idx5, 16) - pick8(c1, idx6, 16)
    return y

@@ -1,0 +1,168 @@
+from contextlib import ExitStack
+
+import concourse.mybir as mybir
+
+D, K, T, I, Q = 512, 512, 1024, 512, 128
+FLOPS = 2 * D * K * Q + 2 * K * T * Q + 2 * D * T * Q
+
+F32 = mybir.dt.float32
+BF16 = mybir.dt.bfloat16
+I32 = mybir.dt.int32
+U32 = mybir.dt.uint32
+U16 = mybir.dt.uint16
+U8 = mybir.dt.uint8
+FP8X4 = mybir.dt.float8_e4m3fn_x4
+FP4X4 = mybir.dt.float4_e2m1fn_x4
+ALU = mybir.AluOpType
+COPY = mybir.ActivationFunctionType.Copy
+
+P = 128
+PACK = 4
+LANES = 16
+SCORE_BANKS = 4
+BANK_COLS = T // SCORE_BANKS
+HALF = I // 2
+
+
+def load_scale_rows(queue, plane, scales):
+    for quad in range(4):
+        queue.dma_start(
+            out=plane[32 * quad : 32 * quad + 4, :].bitcast(I32),
+            in_=scales[0, 4 * quad : 4 * quad + 4, :].bitcast(I32),
+        )
+
+
+def tile_attend_backtrack_madeparts_kernel(
+    tc, states, wq_words, wq_scales, keys_words, keys_scales, tags_words, tags_scales,
+    offs, offs2, offs3, offs4, offs5, offs6, out,
+):
+    nc = tc.nc
+    with ExitStack() as ctx:
+        sb = ctx.enter_context(tc.tile_pool(name="sb", bufs=1))
+        ps = ctx.enter_context(tc.psum_pool(name="ps", bufs=1))
+
+        wq_plane = sb.tile([P, K], U8, align_bytes=64)
+        keys_plane = sb.tile([P, T], U8, align_bytes=64)
+        tags_plane = sb.tile([P, T], U8, align_bytes=64)
+        nc.vector.memset(wq_plane[:].bitcast(I32), 0)
+        nc.gpsimd.memset(tags_plane[:].bitcast(I32), 0)
+        nc.vector.memset(keys_plane[:].bitcast(I32), 0)
+
+        raw = sb.tile([P, PACK, Q], F32)
+        wq_raw = sb.tile([P, K], U32, align_bytes=64)
+        keys = sb.tile([P, T], U32, align_bytes=64)
+        tags = sb.tile([P, 2 * T], U8, align_bytes=64)
+        lists = [sb.tile([P, I // LANES], U16, name="list%d" % n) for n in range(6)]
+        idx, idx2, idx3, idx4, idx5, idx6 = lists
+
+        load_scale_rows(nc.sync, wq_plane, wq_scales)
+        nc.scalar.dma_start(out=raw[:], in_=states.rearrange("(p j) q -> p j q", j=PACK))
+        nc.scalar.dma_start(
+            out=wq_raw[:].bitcast(I32), in_=wq_words[0].rearrange("p n t -> p (n t)").bitcast(I32)
+        )
+        load_scale_rows(nc.gpsimd, tags_plane, tags_scales)
+        nc.sync.dma_start(out=tags[:].bitcast(I32), in_=tags_words[0].bitcast(I32))
+        nc.sync.dma_start(
+            out=keys[:].bitcast(I32), in_=keys_words[0].rearrange("p n t -> p (n t)").bitcast(I32)
+        )
+        load_scale_rows(nc.sync, keys_plane, keys_scales)
+        for tile, source in zip(lists, (offs, offs2, offs3, offs4, offs5, offs6)):
+            nc.sync.dma_start(tile[:], source)
+
+        f1 = sb.tile([P, T], F32)
+        f2 = sb.tile([P, T], F32)
+        nc.vector.memset(f1[:], 0.0)
+        nc.vector.memset(f2[:], 0.0)
+
+        wq_dealt_plane = sb.tile([P, K], U8, align_bytes=64)
+        nc.vector.tensor_copy(
+            out=wq_dealt_plane[:].rearrange("p (t m) -> p m t", t=PACK),
+            in_=wq_plane[:].rearrange("p (m t) -> p m t", t=PACK),
+        )
+        wq_dealt = sb.tile([P, K], U32, align_bytes=64)
+        nc.scalar.copy(
+            out=wq_dealt[:].rearrange("p (t m) -> p m t", t=PACK),
+            in_=wq_raw[:].rearrange("p (m t) -> p m t", t=PACK),
+        )
+
+        st_bf = sb.tile([P, Q, PACK], BF16, align_bytes=64)
+        nc.vector.tensor_copy(out=st_bf[:], in_=raw[:].rearrange("p j q -> p q j"))
+        st_codes = sb.tile([P, Q], U32, align_bytes=64)
+        st_plane = sb.tile([P, Q], U8, align_bytes=64)
+        nc.vector.quantize_mx(
+            out=st_codes[:].bitcast(FP8X4), scales=st_plane[:], in_=st_bf[:].rearrange("p q j -> p (q j)")
+        )
+
+        qv_bank = ps.tile([P, PACK, Q], F32)
+        for t in range(PACK):
+            cols = slice(t * P, (t + 1) * P)
+            nc.tensor.matmul_mx(
+                out=qv_bank[:, t, :],
+                lhsT=wq_dealt[:, cols].bitcast(FP8X4), lhsT_scale=wq_dealt_plane[:, cols],
+                rhs=st_codes[:].bitcast(FP8X4), rhs_scale=st_plane[:],
+                start=True, stop=True,
+            )
+        banks = [ps.tile([P, BANK_COLS], F32, name="score%d" % b) for b in range(SCORE_BANKS)]
+        for b in range(SCORE_BANKS):
+            cols = slice(b * BANK_COLS, (b + 1) * BANK_COLS)
+            nc.tensor.matmul_mx(
+                out=banks[b][:],
+                lhsT=st_codes[:].bitcast(FP8X4), lhsT_scale=st_plane[:],
+                rhs=tags[:, 2 * cols.start : 2 * cols.stop].bitcast(FP4X4), rhs_scale=tags_plane[:, cols],
+                start=True, stop=False,
+            )
+
+        qv_bf = sb.tile([P, Q, PACK], BF16, align_bytes=64)
+        nc.vector.tensor_copy(out=qv_bf[:], in_=qv_bank[:].rearrange("p t q -> p q t"))
+        qv_codes = sb.tile([P, Q], U32, align_bytes=64)
+        qv_plane = sb.tile([P, Q], U8, align_bytes=64)
+        nc.vector.quantize_mx(
+            out=qv_codes[:].bitcast(FP8X4), scales=qv_plane[:], in_=qv_bf[:].rearrange("p q t -> p (q t)")
+        )
+
+        a = sb.tile([P, T], F32)
+        for b in range(SCORE_BANKS):
+            cols = slice(b * BANK_COLS, (b + 1) * BANK_COLS)
+            nc.tensor.matmul_mx(
+                out=banks[b][:],
+                lhsT=qv_codes[:].bitcast(FP8X4), lhsT_scale=qv_plane[:],
+                rhs=keys[:, cols].bitcast(FP8X4), rhs_scale=keys_plane[:, cols],
+                start=False, stop=True,
+            )
+            if b % 2 == 0:
+                nc.vector.tensor_copy(out=a[:, cols], in_=banks[b][:])
+            else:
+                nc.scalar.copy(out=a[:, cols], in_=banks[b][:])
+
+        first, second = slice(0, HALF), slice(HALF, I)
+
+        def part(offsets, slots):
+            return offsets[:, slots.start // LANES : slots.stop // LANES]
+
+        picked = sb.tile([P, I], F32)
+        nc.vector.tensor_copy(out=picked[:, first], in_=a[:].indirect(part(idx, first)))
+        nc.scalar.activation(picked[:, second], a[:].indirect(part(idx, second)), COPY)
+        for slots in (first, second):
+            nc.vector.tensor_copy(out=f1[:].indirect(part(idx2, slots)), in_=picked[:, slots])
+        c1 = sb.tile([P, T], F32)
+        nc.vector.tensor_tensor(c1[:], a[:], f1[:], ALU.subtract)
+
+        left = sb.tile([P, I], F32)
+        w = sb.tile([P, I], F32)
+        nc.vector.tensor_copy(out=left[:, first], in_=c1[:].indirect(part(idx3, first)))
+        nc.scalar.activation(left[:, second], c1[:].indirect(part(idx3, second)), COPY)
+        before = sb.tile([P, I], F32)
+        nc.scalar.activation(before[:], c1[:].indirect(idx6[:]), COPY)
+        for slots in (first, second):
+            nc.vector.tensor_tensor(w[:, slots], left[:, slots], picked[:, slots], ALU.max)
+            nc.vector.tensor_copy(out=f2[:].indirect(part(idx4, slots)), in_=w[:, slots])
+        c2 = sb.tile([P, T], F32)
+        nc.vector.tensor_tensor(c2[:], c1[:], f2[:], ALU.add)
+
+        result = sb.tile([P, I], F32)
+        after = sb.tile([P, HALF], F32)
+        nc.scalar.activation(after[:], c2[:].indirect(part(idx5, second)), COPY)
+        nc.vector.tensor_tensor(result[:, first], c2[:].indirect(part(idx5, first)), before[:, first], ALU.subtract)
+        nc.sync.dma_start(out=out[:, first], in_=result[:, first])
+        nc.vector.tensor_tensor(result[:, second], after[:], before[:, second], ALU.subtract)
+        nc.scalar.dma_start(out=out[:, second], in_=result[:, second])

@@ -19,13 +19,14 @@ COPY = mybir.ActivationFunctionType.Copy
 P = 128
 PACK = 4
 LANES = 16
-SCORE_BANKS = 4
-BANK_COLS = T // SCORE_BANKS
+BANK_EDGES = (0, 256, 512, 768, 896, 1024)
+SHARED = 768
 HALF = I // 2
+LEAD = 128
 
 
-def load_scale_rows(queue, plane, scales):
-    for quad in range(4):
+def load_scale_rows(queue, plane, scales, quads):
+    for quad in quads:
         queue.dma_start(
             out=plane[32 * quad : 32 * quad + 4, :].bitcast(I32),
             in_=scales[0, 4 * quad : 4 * quad + 4, :].bitcast(I32),
@@ -41,11 +42,11 @@ def tile_attend_backtrack_madeparts_kernel(
         sb = ctx.enter_context(tc.tile_pool(name="sb", bufs=1))
         ps = ctx.enter_context(tc.psum_pool(name="ps", bufs=1))
 
-        wq_plane = sb.tile([P, K], U8, align_bytes=64)
+        wq_plane = sb.tile([P, K], U8, align_bytes=64, tag="first")
         keys_plane = sb.tile([P, T], U8, align_bytes=64)
         tags_plane = sb.tile([P, T], U8, align_bytes=64)
-        nc.vector.memset(wq_plane[:].bitcast(I32), 0)
-        nc.gpsimd.memset(tags_plane[:].bitcast(I32), 0)
+        nc.gpsimd.memset(wq_plane[:].bitcast(I32), 0)
+        nc.vector.memset(tags_plane[:].bitcast(I32), 0)
         nc.vector.memset(keys_plane[:].bitcast(I32), 0)
 
         raw = sb.tile([P, PACK, Q], F32)
@@ -55,35 +56,23 @@ def tile_attend_backtrack_madeparts_kernel(
         lists = [sb.tile([P, I // LANES], U16, name="list%d" % n) for n in range(6)]
         idx, idx2, idx3, idx4, idx5, idx6 = lists
 
-        load_scale_rows(nc.sync, wq_plane, wq_scales)
-        nc.scalar.dma_start(out=raw[:], in_=states.rearrange("(p j) q -> p j q", j=PACK))
-        nc.scalar.dma_start(
+        nc.sync.dma_start(out=raw[:], in_=states.rearrange("(p j) q -> p j q", j=PACK))
+        nc.sync.dma_start(
             out=wq_raw[:].bitcast(I32), in_=wq_words[0].rearrange("p n t -> p (n t)").bitcast(I32)
         )
-        load_scale_rows(nc.gpsimd, tags_plane, tags_scales)
+        load_scale_rows(nc.sync, wq_plane, wq_scales, range(4))
         nc.sync.dma_start(out=tags[:].bitcast(I32), in_=tags_words[0].bitcast(I32))
         nc.sync.dma_start(
             out=keys[:].bitcast(I32), in_=keys_words[0].rearrange("p n t -> p (n t)").bitcast(I32)
         )
-        load_scale_rows(nc.sync, keys_plane, keys_scales)
-        for tile, source in zip(lists, (offs, offs2, offs3, offs4, offs5, offs6)):
+        load_scale_rows(nc.gpsimd, tags_plane, tags_scales, range(2, 4))
+        load_scale_rows(nc.sync, tags_plane, tags_scales, range(2))
+        load_scale_rows(nc.sync, keys_plane, keys_scales, range(4))
+        for tile, source in zip((idx, idx2, idx3, idx6, idx4, idx5), (offs, offs2, offs3, offs6, offs4, offs5)):
             nc.sync.dma_start(tile[:], source)
 
-        f1 = sb.tile([P, T], F32)
-        f2 = sb.tile([P, T], F32)
-        nc.vector.memset(f1[:], 0.0)
-        nc.vector.memset(f2[:], 0.0)
-
-        wq_dealt_plane = sb.tile([P, K], U8, align_bytes=64)
-        nc.vector.tensor_copy(
-            out=wq_dealt_plane[:].rearrange("p (t m) -> p m t", t=PACK),
-            in_=wq_plane[:].rearrange("p (m t) -> p m t", t=PACK),
-        )
-        wq_dealt = sb.tile([P, K], U32, align_bytes=64)
-        nc.scalar.copy(
-            out=wq_dealt[:].rearrange("p (t m) -> p m t", t=PACK),
-            in_=wq_raw[:].rearrange("p (m t) -> p m t", t=PACK),
-        )
+        ones = sb.tile([P, LEAD], F32)
+        nc.vector.memset(ones[:], 1.0)
 
         st_bf = sb.tile([P, Q, PACK], BF16, align_bytes=64)
         nc.vector.tensor_copy(out=st_bf[:], in_=raw[:].rearrange("p j q -> p q j"))
@@ -93,6 +82,20 @@ def tile_attend_backtrack_madeparts_kernel(
             out=st_codes[:].bitcast(FP8X4), scales=st_plane[:], in_=st_bf[:].rearrange("p q j -> p (q j)")
         )
 
+        wq_dealt_plane = sb.tile([P, K], U8, align_bytes=64)
+        wq_dealt = sb.tile([P, K], U32, align_bytes=64)
+        for pair in (slice(0, 2), slice(2, 4)):
+            nc.vector.tensor_copy(
+                out=wq_dealt_plane[:].rearrange("p (t m) -> p t m", t=PACK)[:, pair, :],
+                in_=wq_plane[:].rearrange("p (m t) -> p t m", t=PACK)[:, pair, :],
+            )
+            nc.scalar.copy(
+                out=wq_dealt[:].rearrange("p (t m) -> p m t", t=PACK)[:, :, pair],
+                in_=wq_raw[:].rearrange("p (m t) -> p m t", t=PACK)[:, :, pair],
+            )
+
+        f1 = sb.tile([P, T], F32, align_bytes=64, tag="first")
+        nc.vector.memset(f1[:], 0.0)
         qv_bank = ps.tile([P, PACK, Q], F32)
         for t in range(PACK):
             cols = slice(t * P, (t + 1) * P)
@@ -102,9 +105,9 @@ def tile_attend_backtrack_madeparts_kernel(
                 rhs=st_codes[:].bitcast(FP8X4), rhs_scale=st_plane[:],
                 start=True, stop=True,
             )
-        banks = [ps.tile([P, BANK_COLS], F32, name="score%d" % b) for b in range(SCORE_BANKS)]
-        for b in range(SCORE_BANKS):
-            cols = slice(b * BANK_COLS, (b + 1) * BANK_COLS)
+        bank_cols = [slice(lo, hi) for lo, hi in zip(BANK_EDGES, BANK_EDGES[1:])]
+        banks = [ps.tile([P, cols.stop - cols.start], F32, name="score%d" % b) for b, cols in enumerate(bank_cols)]
+        for b, cols in enumerate(bank_cols):
             nc.tensor.matmul_mx(
                 out=banks[b][:],
                 lhsT=st_codes[:].bitcast(FP8X4), lhsT_scale=st_plane[:],
@@ -112,7 +115,7 @@ def tile_attend_backtrack_madeparts_kernel(
                 start=True, stop=False,
             )
 
-        qv_bf = sb.tile([P, Q, PACK], BF16, align_bytes=64)
+        qv_bf = sb.tile([P, Q, PACK], BF16, align_bytes=64, tag="second")
         nc.vector.tensor_copy(out=qv_bf[:], in_=qv_bank[:].rearrange("p t q -> p q t"))
         qv_codes = sb.tile([P, Q], U32, align_bytes=64)
         qv_plane = sb.tile([P, Q], U8, align_bytes=64)
@@ -120,9 +123,10 @@ def tile_attend_backtrack_madeparts_kernel(
             out=qv_codes[:].bitcast(FP8X4), scales=qv_plane[:], in_=qv_bf[:].rearrange("p q t -> p (q t)")
         )
 
+        f2 = sb.tile([P, T], F32, align_bytes=64, tag="second")
+        nc.vector.memset(f2[:], 0.0)
         a = sb.tile([P, T], F32)
-        for b in range(SCORE_BANKS):
-            cols = slice(b * BANK_COLS, (b + 1) * BANK_COLS)
+        for b, cols in enumerate(bank_cols):
             nc.tensor.matmul_mx(
                 out=banks[b][:],
                 lhsT=qv_codes[:].bitcast(FP8X4), lhsT_scale=qv_plane[:],
@@ -140,12 +144,16 @@ def tile_attend_backtrack_madeparts_kernel(
             return offsets[:, slots.start // LANES : slots.stop // LANES]
 
         picked = sb.tile([P, I], F32)
-        nc.vector.tensor_copy(out=picked[:, first], in_=a[:].indirect(part(idx, first)))
-        nc.scalar.activation(picked[:, second], a[:].indirect(part(idx, second)), COPY)
-        for slots in (first, second):
+        lead, rest = slice(0, LEAD), slice(LEAD, I)
+        nc.vector.tensor_tensor(picked[:, lead], a[:].indirect(part(idx, lead)), ones[:], ALU.mult)
+        nc.scalar.activation(picked[:, rest], a[:].indirect(part(idx, rest)), COPY)
+        for slots in (lead, rest):
             nc.vector.tensor_copy(out=f1[:].indirect(part(idx2, slots)), in_=picked[:, slots])
         c1 = sb.tile([P, T], F32)
-        nc.vector.tensor_tensor(c1[:], a[:], f1[:], ALU.subtract)
+        for b, cols in enumerate(bank_cols):
+            if cols.stop <= SHARED:
+                nc.vector.tensor_tensor(c1[:, cols], banks[b][:], f1[:, cols], ALU.subtract)
+        nc.gpsimd.tensor_tensor(c1[:, SHARED:], a[:, SHARED:], f1[:, SHARED:], ALU.subtract)
 
         left = sb.tile([P, I], F32)
         w = sb.tile([P, I], F32)
@@ -155,6 +163,7 @@ def tile_attend_backtrack_madeparts_kernel(
         nc.scalar.activation(before[:], c1[:].indirect(idx6[:]), COPY)
         for slots in (first, second):
             nc.vector.tensor_tensor(w[:, slots], left[:, slots], picked[:, slots], ALU.max)
+        for slots in (first, second):
             nc.vector.tensor_copy(out=f2[:].indirect(part(idx4, slots)), in_=w[:, slots])
         c2 = sb.tile([P, T], F32)
         nc.vector.tensor_tensor(c2[:], c1[:], f2[:], ALU.add)

@@ -1,6 +1,7 @@
 from contextlib import ExitStack
 
 import concourse.mybir as mybir
+from concourse.masks import make_identity
 
 D, K, T, I, Q = 512, 512, 1024, 512, 128
 FLOPS = 2 * D * K * Q + 2 * K * T * Q + 2 * D * T * Q
@@ -51,7 +52,7 @@ def tile_attend_backtrack_madeparts_kernel(
 
         raw = sb.tile([P, PACK, Q], F32)
         wq_raw = sb.tile([P, K], U32, align_bytes=64)
-        keys = sb.tile([P, T], U32, align_bytes=64)
+        keys = [sb.tile([P, T // 2], U32, align_bytes=64, name="keys%d" % h) for h in range(2)]
         tags = sb.tile([P, 2 * T], U8, align_bytes=64)
         lists = [sb.tile([P, I // LANES], U16, name="list%d" % n) for n in range(6)]
         idx, idx2, idx3, idx4, idx5, idx6 = lists
@@ -62,12 +63,15 @@ def tile_attend_backtrack_madeparts_kernel(
         )
         load_scale_rows(nc.sync, wq_plane, wq_scales, range(4))
         nc.sync.dma_start(out=tags[:].bitcast(I32), in_=tags_words[0].bitcast(I32))
-        nc.sync.dma_start(
-            out=keys[:].bitcast(I32), in_=keys_words[0].rearrange("p n t -> p (n t)").bitcast(I32)
-        )
         load_scale_rows(nc.gpsimd, tags_plane, tags_scales, range(2, 4))
+        identity = sb.tile([P, P], F32)
+        nc.vector.memset(identity[:], 0.0)
+        make_identity(nc, identity[:], nomemset=True)
         load_scale_rows(nc.sync, tags_plane, tags_scales, range(2))
+        keys_rows = keys_words[0].rearrange("p n t -> p (n t)").bitcast(I32)
+        nc.sync.dma_start(out=keys[0][:].bitcast(I32), in_=keys_rows[:, : T // 2])
         load_scale_rows(nc.sync, keys_plane, keys_scales, range(4))
+        nc.sync.dma_start(out=keys[1][:].bitcast(I32), in_=keys_rows[:, T // 2 :])
         for tile, source in zip((idx, idx2, idx3, idx6, idx4, idx5), (offs, offs2, offs3, offs6, offs4, offs5)):
             nc.sync.dma_start(tile[:], source)
 
@@ -130,7 +134,7 @@ def tile_attend_backtrack_madeparts_kernel(
             nc.tensor.matmul_mx(
                 out=banks[b][:],
                 lhsT=qv_codes[:].bitcast(FP8X4), lhsT_scale=qv_plane[:],
-                rhs=keys[:, cols].bitcast(FP8X4), rhs_scale=keys_plane[:, cols],
+                rhs=keys[cols.start // (T // 2)][:, cols.start % (T // 2) : (cols.stop - 1) % (T // 2) + 1].bitcast(FP8X4), rhs_scale=keys_plane[:, cols],
                 start=False, stop=True,
             )
             if b % 2 == 0:
@@ -155,23 +159,39 @@ def tile_attend_backtrack_madeparts_kernel(
                 nc.vector.tensor_tensor(c1[:, cols], banks[b][:], f1[:, cols], ALU.subtract)
         nc.gpsimd.tensor_tensor(c1[:, SHARED:], a[:, SHARED:], f1[:, SHARED:], ALU.subtract)
 
-        left = sb.tile([P, I], F32)
-        w = sb.tile([P, I], F32)
-        nc.vector.tensor_copy(out=left[:, first], in_=c1[:].indirect(part(idx3, first)))
-        nc.scalar.activation(left[:, second], c1[:].indirect(part(idx3, second)), COPY)
+        left = [sb.tile([P, HALF], F32, name="left%d" % h) for h in range(2)]
+        w = [sb.tile([P, HALF], F32, name="w%d" % h) for h in range(2)]
+        nc.vector.tensor_copy(out=left[0][:], in_=c1[:].indirect(part(idx3, first)))
+        nc.scalar.activation(left[1][:], c1[:].indirect(part(idx3, second)), COPY)
+        c1_turned = sb.tile([P, SHARED], F32)
+        c1_banks = []
+        for cols, tag in ((slice(0, 512), "qv_bank"), (slice(512, SHARED), "score4")):
+            width = cols.stop - cols.start
+            turned = ps.tile([P, width], F32, name="turned", tag=tag)
+            for lo in range(0, width, P):
+                nc.tensor.transpose(turned[:, lo : lo + P], c1[:, cols.start + lo : cols.start + lo + P], identity[:])
+            nc.scalar.copy(out=c1_turned[:, cols], in_=turned[:])
+        for cols in (slice(0, 512), slice(512, SHARED)):
+            width = cols.stop - cols.start
+            back = ps.tile([P, width], F32, name="back%d" % cols.start)
+            for lo in range(0, width, P):
+                nc.tensor.transpose(back[:, lo : lo + P], c1_turned[:, cols.start + lo : cols.start + lo + P], identity[:])
+            c1_banks.append((cols, back))
         before = sb.tile([P, I], F32)
         nc.scalar.activation(before[:], c1[:].indirect(idx6[:]), COPY)
-        for slots in (first, second):
-            nc.vector.tensor_tensor(w[:, slots], left[:, slots], picked[:, slots], ALU.max)
-        for slots in (first, second):
-            nc.vector.tensor_copy(out=f2[:].indirect(part(idx4, slots)), in_=w[:, slots])
+        for h, slots in enumerate((first, second)):
+            nc.vector.tensor_tensor(w[h][:], left[h][:], picked[:, slots], ALU.max)
+        for h, slots in enumerate((first, second)):
+            nc.vector.tensor_copy(out=f2[:].indirect(part(idx4, slots)), in_=w[h][:])
         c2 = sb.tile([P, T], F32)
-        nc.vector.tensor_tensor(c2[:], c1[:], f2[:], ALU.add)
+        for cols, back in c1_banks:
+            nc.vector.tensor_tensor(c2[:, cols], back[:], f2[:, cols], ALU.add)
+        nc.gpsimd.tensor_tensor(c2[:, SHARED:], c1[:, SHARED:], f2[:, SHARED:], ALU.add)
 
-        result = sb.tile([P, I], F32)
+        result = [sb.tile([P, HALF], F32, name="result%d" % h) for h in range(2)]
         after = sb.tile([P, HALF], F32)
         nc.scalar.activation(after[:], c2[:].indirect(part(idx5, second)), COPY)
-        nc.vector.tensor_tensor(result[:, first], c2[:].indirect(part(idx5, first)), before[:, first], ALU.subtract)
-        nc.sync.dma_start(out=out[:, first], in_=result[:, first])
-        nc.vector.tensor_tensor(result[:, second], after[:], before[:, second], ALU.subtract)
-        nc.scalar.dma_start(out=out[:, second], in_=result[:, second])
+        nc.vector.tensor_tensor(result[0][:], c2[:].indirect(part(idx5, first)), before[:, first], ALU.subtract)
+        nc.sync.dma_start(out=out[:, first], in_=result[0][:])
+        nc.vector.tensor_tensor(result[1][:], after[:], before[:, second], ALU.subtract)
+        nc.scalar.dma_start(out=out[:, second], in_=result[1][:])

from contextlib import ExitStack

import concourse.mybir as mybir
from concourse.masks import make_identity

D, K, T, I, Q = 512, 512, 1024, 512, 128
FLOPS = 2 * D * K * Q + 2 * K * T * Q + 2 * D * T * Q

F32 = mybir.dt.float32
BF16 = mybir.dt.bfloat16
I32 = mybir.dt.int32
U32 = mybir.dt.uint32
U16 = mybir.dt.uint16
U8 = mybir.dt.uint8
FP8X4 = mybir.dt.float8_e4m3fn_x4
FP4X4 = mybir.dt.float4_e2m1fn_x4
ALU = mybir.AluOpType
COPY = mybir.ActivationFunctionType.Copy

P = 128
PACK = 4
LANES = 16
BANK_EDGES = (0, 256, 512, 768, 896, 1024)
SHARED = 768
HALF = I // 2
LEAD = 128


def load_scale_rows(queue, plane, scales, quads):
    for quad in quads:
        queue.dma_start(
            out=plane[32 * quad : 32 * quad + 4, :].bitcast(I32),
            in_=scales[0, 4 * quad : 4 * quad + 4, :].bitcast(I32),
        )


def tile_attend_backtrack_madeparts_kernel(
    tc, states, wq_words, wq_scales, keys_words, keys_scales, tags_words, tags_scales,
    offs, offs2, offs3, offs4, offs5, offs6, out,
):
    nc = tc.nc
    with ExitStack() as ctx:
        sb = ctx.enter_context(tc.tile_pool(name="sb", bufs=1))
        ps = ctx.enter_context(tc.psum_pool(name="ps", bufs=1))

        wq_plane = sb.tile([P, K], U8, align_bytes=64, tag="first")
        keys_plane = sb.tile([P, T], U8, align_bytes=64)
        tags_plane = sb.tile([P, T], U8, align_bytes=64)
        nc.gpsimd.memset(wq_plane[:].bitcast(I32), 0)
        nc.vector.memset(tags_plane[:].bitcast(I32), 0)
        nc.vector.memset(keys_plane[:].bitcast(I32), 0)

        raw = sb.tile([P, PACK, Q], F32)
        wq_raw = sb.tile([P, K], U32, align_bytes=64)
        keys = [sb.tile([P, T // 2], U32, align_bytes=64, name="keys%d" % h) for h in range(2)]
        tags = sb.tile([P, 2 * T], U8, align_bytes=64)
        lists = [sb.tile([P, I // LANES], U16, name="list%d" % n) for n in range(6)]
        idx, idx2, idx3, idx4, idx5, idx6 = lists

        nc.sync.dma_start(out=raw[:], in_=states.rearrange("(p j) q -> p j q", j=PACK))
        nc.sync.dma_start(
            out=wq_raw[:].bitcast(I32), in_=wq_words[0].rearrange("p n t -> p (n t)").bitcast(I32)
        )
        load_scale_rows(nc.sync, wq_plane, wq_scales, range(4))
        nc.sync.dma_start(out=tags[:].bitcast(I32), in_=tags_words[0].bitcast(I32))
        load_scale_rows(nc.gpsimd, tags_plane, tags_scales, range(2, 4))
        identity = sb.tile([P, P], F32)
        nc.vector.memset(identity[:], 0.0)
        make_identity(nc, identity[:], nomemset=True)
        load_scale_rows(nc.sync, tags_plane, tags_scales, range(2))
        keys_rows = keys_words[0].rearrange("p n t -> p (n t)").bitcast(I32)
        nc.sync.dma_start(out=keys[0][:].bitcast(I32), in_=keys_rows[:, : T // 2])
        load_scale_rows(nc.sync, keys_plane, keys_scales, range(4))
        nc.sync.dma_start(out=keys[1][:].bitcast(I32), in_=keys_rows[:, T // 2 :])
        for tile, source in zip((idx, idx2, idx3, idx6, idx4, idx5), (offs, offs2, offs3, offs6, offs4, offs5)):
            nc.sync.dma_start(tile[:], source)

        ones = sb.tile([P, LEAD], F32)
        nc.vector.memset(ones[:], 1.0)

        st_bf = sb.tile([P, Q, PACK], BF16, align_bytes=64)
        nc.vector.tensor_copy(out=st_bf[:], in_=raw[:].rearrange("p j q -> p q j"))
        st_codes = sb.tile([P, Q], U32, align_bytes=64)
        st_plane = sb.tile([P, Q], U8, align_bytes=64)
        nc.vector.quantize_mx(
            out=st_codes[:].bitcast(FP8X4), scales=st_plane[:], in_=st_bf[:].rearrange("p q j -> p (q j)")
        )

        wq_dealt_plane = sb.tile([P, K], U8, align_bytes=64)
        wq_dealt = sb.tile([P, K], U32, align_bytes=64)
        for pair in (slice(0, 2), slice(2, 4)):
            nc.vector.tensor_copy(
                out=wq_dealt_plane[:].rearrange("p (t m) -> p t m", t=PACK)[:, pair, :],
                in_=wq_plane[:].rearrange("p (m t) -> p t m", t=PACK)[:, pair, :],
            )
            nc.scalar.copy(
                out=wq_dealt[:].rearrange("p (t m) -> p m t", t=PACK)[:, :, pair],
                in_=wq_raw[:].rearrange("p (m t) -> p m t", t=PACK)[:, :, pair],
            )

        f1 = sb.tile([P, T], F32, align_bytes=64, tag="first")
        nc.vector.memset(f1[:], 0.0)
        qv_bank = ps.tile([P, PACK, Q], F32)
        for t in range(PACK):
            cols = slice(t * P, (t + 1) * P)
            nc.tensor.matmul_mx(
                out=qv_bank[:, t, :],
                lhsT=wq_dealt[:, cols].bitcast(FP8X4), lhsT_scale=wq_dealt_plane[:, cols],
                rhs=st_codes[:].bitcast(FP8X4), rhs_scale=st_plane[:],
                start=True, stop=True,
            )
        bank_cols = [slice(lo, hi) for lo, hi in zip(BANK_EDGES, BANK_EDGES[1:])]
        banks = [ps.tile([P, cols.stop - cols.start], F32, name="score%d" % b) for b, cols in enumerate(bank_cols)]
        for b, cols in enumerate(bank_cols):
            nc.tensor.matmul_mx(
                out=banks[b][:],
                lhsT=st_codes[:].bitcast(FP8X4), lhsT_scale=st_plane[:],
                rhs=tags[:, 2 * cols.start : 2 * cols.stop].bitcast(FP4X4), rhs_scale=tags_plane[:, cols],
                start=True, stop=False,
            )

        qv_bf = sb.tile([P, Q, PACK], BF16, align_bytes=64, tag="second")
        nc.vector.tensor_copy(out=qv_bf[:], in_=qv_bank[:].rearrange("p t q -> p q t"))
        qv_codes = sb.tile([P, Q], U32, align_bytes=64)
        qv_plane = sb.tile([P, Q], U8, align_bytes=64)
        nc.vector.quantize_mx(
            out=qv_codes[:].bitcast(FP8X4), scales=qv_plane[:], in_=qv_bf[:].rearrange("p q t -> p (q t)")
        )

        f2 = sb.tile([P, T], F32, align_bytes=64, tag="second")
        nc.vector.memset(f2[:], 0.0)
        a = sb.tile([P, T], F32)
        for b, cols in enumerate(bank_cols):
            nc.tensor.matmul_mx(
                out=banks[b][:],
                lhsT=qv_codes[:].bitcast(FP8X4), lhsT_scale=qv_plane[:],
                rhs=keys[cols.start // (T // 2)][:, cols.start % (T // 2) : (cols.stop - 1) % (T // 2) + 1].bitcast(FP8X4), rhs_scale=keys_plane[:, cols],
                start=False, stop=True,
            )
            if b % 2 == 0:
                nc.vector.tensor_copy(out=a[:, cols], in_=banks[b][:])
            else:
                nc.scalar.copy(out=a[:, cols], in_=banks[b][:])

        first, second = slice(0, HALF), slice(HALF, I)

        def part(offsets, slots):
            return offsets[:, slots.start // LANES : slots.stop // LANES]

        picked = sb.tile([P, I], F32)
        lead, rest = slice(0, LEAD), slice(LEAD, I)
        nc.vector.tensor_tensor(picked[:, lead], a[:].indirect(part(idx, lead)), ones[:], ALU.mult)
        nc.scalar.activation(picked[:, rest], a[:].indirect(part(idx, rest)), COPY)
        for slots in (lead, rest):
            nc.vector.tensor_copy(out=f1[:].indirect(part(idx2, slots)), in_=picked[:, slots])
        c1 = sb.tile([P, T], F32)
        for b, cols in enumerate(bank_cols):
            if cols.stop <= SHARED:
                nc.vector.tensor_tensor(c1[:, cols], banks[b][:], f1[:, cols], ALU.subtract)
        nc.gpsimd.tensor_tensor(c1[:, SHARED:], a[:, SHARED:], f1[:, SHARED:], ALU.subtract)

        left = [sb.tile([P, HALF], F32, name="left%d" % h) for h in range(2)]
        w = [sb.tile([P, HALF], F32, name="w%d" % h) for h in range(2)]
        nc.vector.tensor_copy(out=left[0][:], in_=c1[:].indirect(part(idx3, first)))
        nc.scalar.activation(left[1][:], c1[:].indirect(part(idx3, second)), COPY)
        c1_turned = sb.tile([P, SHARED], F32)
        c1_banks = []
        for cols, tag in ((slice(0, 512), "qv_bank"), (slice(512, SHARED), "score4")):
            width = cols.stop - cols.start
            turned = ps.tile([P, width], F32, name="turned", tag=tag)
            for lo in range(0, width, P):
                nc.tensor.transpose(turned[:, lo : lo + P], c1[:, cols.start + lo : cols.start + lo + P], identity[:])
            nc.scalar.copy(out=c1_turned[:, cols], in_=turned[:])
        for cols in (slice(0, 512), slice(512, SHARED)):
            width = cols.stop - cols.start
            back = ps.tile([P, width], F32, name="back%d" % cols.start)
            for lo in range(0, width, P):
                nc.tensor.transpose(back[:, lo : lo + P], c1_turned[:, cols.start + lo : cols.start + lo + P], identity[:])
            c1_banks.append((cols, back))
        before = sb.tile([P, I], F32)
        nc.scalar.activation(before[:], c1[:].indirect(idx6[:]), COPY)
        for h, slots in enumerate((first, second)):
            nc.vector.tensor_tensor(w[h][:], left[h][:], picked[:, slots], ALU.max)
        for h, slots in enumerate((first, second)):
            nc.vector.tensor_copy(out=f2[:].indirect(part(idx4, slots)), in_=w[h][:])
        c2 = sb.tile([P, T], F32)
        for cols, back in c1_banks:
            nc.vector.tensor_tensor(c2[:, cols], back[:], f2[:, cols], ALU.add)
        nc.gpsimd.tensor_tensor(c2[:, SHARED:], c1[:, SHARED:], f2[:, SHARED:], ALU.add)

        result = [sb.tile([P, HALF], F32, name="result%d" % h) for h in range(2)]
        after = sb.tile([P, HALF], F32)
        nc.scalar.activation(after[:], c2[:].indirect(part(idx5, second)), COPY)
        nc.vector.tensor_tensor(result[0][:], c2[:].indirect(part(idx5, first)), before[:, first], ALU.subtract)
        nc.sync.dma_start(out=out[:, first], in_=result[0][:])
        nc.vector.tensor_tensor(result[1][:], after[:], before[:, second], ALU.subtract)
        nc.scalar.dma_start(out=out[:, second], in_=result[1][:])
